import numpy as np, ml_dtypes
CORES = [23,119,17,113]
N = 4
T, KB = 2048, 16
def entries(a): return a.T.reshape(-1)
def pack(v, P): return np.ascontiguousarray(np.asarray(v, np.int32).reshape(-1, P).T)
def order(K):
    return np.argsort(K, kind="stable")
def lists(rng, how):
    K = rng.integers(0, KB, (N, T)); i = np.arange(N)
    if how == "astride":
        s, m, k = rng.integers(1, N), rng.integers(T // 4, 3 * T // 4), np.sort(rng.permutation(KB)[:3])
        K = np.repeat(np.where(i >= s, k[1], k[2])[:, None], T, axis=1); K[s - 1, rng.permutation(T)[:m]] = k[0]
    if how == "skew": K = np.stack([rng.choice(KB, T, p=rng.dirichlet(np.ones(KB) * 0.5)) for r in range(N)])
    if how[:4] == "turn":
        s = rng.choice(i[1:][ord(how[-1]) - 97::3]); K = ((i + s) % N * KB // N)[:, None] + rng.integers(0, max(KB // N, 1), (N, T))
    return {"key": np.stack([pack(k, 16) for k in K])}
def setup_inputs(rng):
    return dict({"x": rng.standard_normal((N, 128, T), dtype=np.float32).astype(ml_dtypes.bfloat16)}, **lists(rng, "uniform"))
def setup_inputs_astride(rng):
    d = setup_inputs(rng); d.update(lists(rng, "astride"))
    for k in ("x",): d[k] = (d[k].astype(np.float32) * 1048576.0).astype(d[k].dtype)
    return d
def setup_inputs_skew(rng):
    d = setup_inputs(rng); d.update(lists(rng, "skew"))
    for k in ("x",): d[k] = (d[k].astype(np.float32) * (1 / 1024.0)).astype(d[k].dtype)
    return d
def setup_inputs_turna(rng):
    d = setup_inputs(rng); d.update(lists(rng, "turna"))
    return d
def setup_inputs_turnb(rng):
    d = setup_inputs(rng); d.update(lists(rng, "turnb"))
    return d
def setup_inputs_turnc(rng):
    d = setup_inputs(rng); d.update(lists(rng, "turnc"))
    return d
def check_inputs(x):
    bad = []
    if x["key"].min() < 0 or x["key"].max() >= KB: bad.append("key out of range")
    return bad
def reference(x, key):
    X = np.concatenate(list(x), axis=1); K = np.concatenate([entries(a) for a in key])
    Y = X[:, order(K)]
    return {"y": np.stack([Y[:, T * r:T * r + T] for r in range(N)])}

@@ -1,0 +1,241 @@
+from concourse.bass import DstId, RemoteDMATransfer
+from concourse.mybir import AluOpType as A, ActivationFunctionType as F
+
+W = 2048
+NK = 16
+BIG = 16384.0
+CH = [(0, 768), (768, 1536), (1536, 2048)]
+NQ = 4
+
+SCRATCH = {
+    "xw": ("sbuf", [128, 4 * W], "bfloat16"),
+    "hb": ("sbuf", [128, W], "bfloat16"),
+    "yb": ("sbuf", [128, W], "bfloat16"),
+    "win": ("sbuf", [128, 4 * W], "bfloat16"),
+    "kraw": ("sbuf", [16, 128], "int32"),
+    "kb": ("sbuf", [16, 128], "bfloat16"),
+    "kall": ("sbuf", [128, 64], "bfloat16"),
+    "ones": ("sbuf", [128, 240], "bfloat16"),
+    "zb": ("sbuf", [16, 240], "bfloat16"),
+    "tri": ("sbuf", [128, 128], "bfloat16"),
+    "mask8": ("sbuf", [128, 512], "bfloat16"),
+    "pul": ("sbuf", [128, 1024], "bfloat16"),
+    "mask16": ("sbuf", [8, 1024], "bfloat16"),
+    "vi": ("sbuf", [8, 1024], "bfloat16"),
+    "vb": ("sbuf", [8, 1024], "bfloat16"),
+    "val": ("sbuf", [128, 1024], "bfloat16"),
+    "gz": ("sbuf", [128, 144], "bfloat16"),
+    "gw": ("sbuf", [128, 144], "bfloat16"),
+    "pc": ("sbuf", [128, 1], "int32"),
+    "pq": ("sbuf", [128, 1], "int32"),
+    "pc16": ("sbuf", [128, 1], "float32"),
+    "wa": ("sbuf", [128, 1], "float32"),
+    "wb": ("sbuf", [128, 1], "float32"),
+    "wc": ("sbuf", [128, 1], "float32"),
+    "hot": ("sbuf", [128, 1024], "bfloat16"),
+    "run": ("sbuf", [128, 1024], "bfloat16"),
+    "r0": ("sbuf", [128, 512], "float32"),
+    "r1": ("sbuf", [128, 512], "float32"),
+    "pm": ("sbuf", [128, 64], "float32"),
+    "off": ("sbuf", [128, 64], "uint16"),
+    "lst": ("sbuf", [128, 128], "uint16"),
+    "kps": ("psum", [128, 512], "float32"),
+    "z0": ("psum", [128, 512], "float32"),
+    "z1": ("psum", [128, 512], "float32"),
+    "l0": ("psum", [128, 512], "float32"),
+    "l1": ("psum", [128, 512], "float32"),
+}
+SEMAPHORES = (["kl", "ld0", "ld1", "ld2", "kin", "xin", "hin0", "hin1", "sent"]
+              + ["ones_", "tri0", "tri1", "tri2", "zb_", "pc_", "c1", "c2", "v_", "kb_", "kp_", "ko", "vi_", "vb_", "vd",
+                 "win_", "q_", "w_", "w2", "g_", "z0_", "z1_", "r_", "pm_", "off_", "sc", "l0_", "l1_", "d0", "d1",
+                 "gs0", "gs1", "gv0", "gv1", "st", "st2"]
+              + ["i%d" % q for q in range(NQ)] + ["s%d" % q for q in range(NQ)])
+
+
+def dst(topo, c):
+    rid, pid, _ = topo.addr(c)
+    return DstId(rid=rid, pnc=pid)
+
+
+def helper_of(topo, cores, src, far):
+    return [c for c in range(128) if topo.chip(c) == topo.chip(far) and topo.die(c) == topo.die(src)
+            and c not in cores][0]
+
+
+def rank_program(g, core, T, topo):
+    cores = list(T.cores)
+    if T.rank_of(core) is None:
+        helper_program(g, core, T, topo, cores)
+    else:
+        member_program(g, core, T, topo, cores)
+
+
+def helper_program(g, core, T, topo, cores):
+    here = [c for c in cores if topo.chip(c) == topo.chip(core)]
+    if not here:
+        return
+    srcs = [s for s in cores if topo.chip(s) != topo.chip(core) and helper_of(topo, cores, s, here[0]) == core]
+    sem = T.sem
+    n = 0
+    for s in srcs:
+        r = T.rank_of(s)
+        for j, (a, b) in enumerate(CH[:2]):
+            g.wait_ge(sem["hin%d" % j], 8)
+            d = T.xw[:, W * r + a:W * r + b]
+            g.remote_dma_fused([RemoteDMATransfer(
+                src=T.hb[:, a:b], dsts=[d for _ in here], dst_ids=[dst(topo, c) for c in here],
+                dma_engine_mask=topo.mask(core, here[0]), remote_sem=sem.xin)], local_sem=sem.sent)
+            n += 16
+    if n:
+        g.wait_ge(sem.sent, n)
+
+
+def member_program(g, core, T, topo, cores):
+    r = T.rank_of(core)
+    sem = T.sem
+    v, te, sc, sy = g.vector, g.tensor, g.scalar, g.sync
+    mate = [c for c in cores if c != core and topo.chip(c) == topo.chip(core)][0]
+    far = [c for c in cores if topo.chip(c) != topo.chip(core)]
+    helper = helper_of(topo, cores, core, far[0])
+    m_off = topo.mask(core, far[0])
+    m_on = topo.mask(core, mate) & ~m_off
+    n_off, n_on = bin(m_off).count("1"), bin(m_on).count("1")
+    base = W * r
+
+    sc.dma_start(T.kraw[:, :], T.key[:, :]).then_inc(sem.kl, 16)
+    for j, (a, b) in enumerate(CH):
+        sy.dma_start(T.xw[:, base + a:base + b], T.x[:, a:b]).then_inc(sem["ld%d" % j], 16)
+
+    g.wait_ge(sem.ones_, 1)
+    g.affine_select(T.zb[:, :], T.ones[0:16, :], [[1, 240]], A.is_equal, 0.0, -112, -1).then_inc(sem.zb_, 1)
+    g.iota(T.pc[:, :], [[1, 1]], 0, 1).then_inc(sem.pc_, 1)
+    g.iota(T.pc16[:, :], [[1, 1]], 0, 16, allow_small_or_imprecise_dtypes=True).then_inc(sem.pc_, 1)
+    g.wait_ge(sem.tri0, 1)
+    g.affine_select(T.tri[:, :], T.tri[:, :], [[-1, 128]], A.is_gt, 0.0, 0, 1).then_inc(sem.tri1, 1)
+    g.wait_ge(sem.tri1, 1)
+    g.affine_select(T.tri[:, :], T.tri[:, :], [[-1, 128]], A.not_equal, BIG, 0, 1).then_inc(sem.tri2, 1)
+    g.wait_ge(sem.ko, 1)
+    own = T.kall[:, 16 * r:16 * r + 16]
+    g.remote_dma_fused([RemoteDMATransfer(src=own, dsts=[own, own, own], dst_ids=[dst(topo, c) for c in far + [mate]],
+                                          dma_engine_mask=m_off, remote_sem=sem.kin)], local_sem=sem.sent)
+    n = n_off
+    for j, (a, b) in enumerate(CH):
+        g.wait_ge(sem["ld%d" % j], 16)
+        src = T.xw[:, base + a:base + b]
+        if j < 2:
+            t1 = RemoteDMATransfer(src=src, dst=T.hb[:, a:b], dst_ids=[dst(topo, helper)], dma_engine_mask=m_off,
+                                   remote_sem=sem["hin%d" % j])
+        else:
+            t1 = RemoteDMATransfer(src=src, dsts=[src, src], dst_ids=[dst(topo, c) for c in far], dma_engine_mask=m_off,
+                                   remote_sem=sem.xin)
+        t2 = RemoteDMATransfer(src=src, dst=src, dst_ids=[dst(topo, mate)], dma_engine_mask=m_on, remote_sem=sem.xin)
+        g.remote_dma_fused([t1, t2], local_sem=sem.sent)
+        n += n_off + n_on
+    g.wait_ge(sem.sent, n)
+    n_xin = 3 * n_on + 2 * (2 * 16 + n_off)
+
+    v.memset(T.ones[:, :], 1.0).then_inc(sem.ones_, 1)
+    v.memset(T.tri[:, :], -1.0).then_inc(sem.tri0, 1)
+    v.memset(T.mask8[:, :], 1.0).then_inc(sem.c1, 1)
+    v.memset(T.pul[:, :], 0.0).then_inc(sem.c1, 1)
+    v.memset(T.mask16[:, :], 1.0).then_inc(sem.c1, 1)
+    v.memset(T.gz[:, :], 0.0).then_inc(sem.c1, 1)
+    v.wait_ge(sem.c1, 4)
+    v.memset(T.mask8[:, 0:512:8], 0.0).then_inc(sem.c2, 1)
+    v.memset(T.pul[:, 0:1024:16], 1.0).then_inc(sem.c2, 1)
+    v.memset(T.mask16[:, 0:1024:16], 0.0).then_inc(sem.c2, 1)
+    v.memset(T.gz[:, 15:144:16], 1.0).then_inc(sem.c2, 1)
+    v.wait_ge(sem.kl, 16)
+    v.tensor_copy(T.kb[:, :], T.kraw[:, :]).then_inc(sem.kb_, 1)
+    v.wait_ge(sem.c2, 4)
+    v.tensor_tensor_scan(T.val[:, :], T.pul[:, :], T.pul[:, :], 0.0, A.add, A.max).then_inc(sem.v_, 1)
+    v.wait_ge(sem.kp_, 1)
+    v.tensor_copy(own, T.kps[:, 0:16]).then_inc(sem.ko, 1)
+    v.tensor_tensor_scan(T.vi[:, :], T.mask16[:, :], T.mask16[:, :], 0.0, A.mult, A.add).then_inc(sem.vi_, 1)
+    v.wait_ge(sem.pc_, 2)
+    v.tensor_scalar(T.pq[:, :], T.pc[:, :], 15, None, A.bitwise_and).then_inc(sem.q_, 1)
+    v.wait_ge(sem.vi_, 1)
+    v.tensor_scalar(T.vb[:, :], T.vi[:, :], T.pc16[0:8, 0:1], None, A.add).then_inc(sem.vb_, 1)
+    v.wait_ge(sem.q_, 1)
+    v.tensor_scalar(T.wa[:, :], T.pq[:, :], 0.0, 128.0, A.is_equal, A.mult).then_inc(sem.w_, 1)
+    v.tensor_scalar(T.wb[:, :], T.pq[:, :], 1.0, None, A.is_equal).then_inc(sem.w_, 1)
+    v.wait_ge(sem.w_, 2)
+    v.tensor_tensor(T.wc[:, :], T.wa[:, :], T.wb[:, :], A.add).then_inc(sem.w2, 1)
+    v.memset(T.win[:, base:base + W], 0.0).then_inc(sem.win_, 1)
+    v.wait_ge(sem.w2, 1)
+    v.tensor_scalar(T.gw[:, :], T.gz[:, :], T.wc[:, 0:1], None, A.mult).then_inc(sem.g_, 1)
+    v.wait_ge(sem.ko, 1)
+    v.wait_ge(sem.kin, 3 * n_off)
+    kq = NK // NQ
+    for q in range(NQ):
+        for k in range(kq * q, kq * q + kq):
+            v.tensor_scalar(T.hot[:, 64 * k:64 * k + 64], T.kall[:, :], float(k), None, A.is_equal).then_inc(sem["i%d" % q], 1)
+        v.wait_ge(sem["i%d" % q], kq)
+        if q:
+            v.wait_ge(sem["s%d" % (q - 1)], 1)
+        lo, hi = 64 * kq * q, 64 * kq * (q + 1)
+        v.tensor_tensor_scan(T.run[:, lo:hi], T.hot[:, lo:hi], T.hot[:, lo:hi],
+                             T.run[:, lo - 1:lo] if q else 0.0, A.add, A.max).then_inc(sem["s%d" % q], 1)
+    for h in range(2):
+        v.wait_ge(sem["z%d_" % h], 8)
+        v.tensor_tensor_scan(T["r%d" % h][:, :], T.mask8[:, :], T["z%d" % h][:, :], 0.0, A.mult, A.max).then_inc(sem.r_, 1)
+    v.wait_ge(sem.r_, 2)
+    v.tensor_tensor(T.pm[:, :], T.r0[:, 7:512:8], T.r1[:, 7:512:8], A.max).then_inc(sem.pm_, 1)
+    v.wait_ge(sem.pm_, 1)
+    v.tensor_scalar(T.off[:, :], T.pm[:, :], BIG + 1.0, None, A.subtract).then_inc(sem.off_, 1)
+    v.wait_ge(sem.off_, 1)
+    v.wait_ge(sem.win_, 1)
+    v.wait_ge(sem.vd, 16)
+    v.tensor_copy(T.win[:, :].indirect(T.off[:, 0:64]), T.val[:, :]).then_inc(sem.sc, 1)
+    for h in range(2):
+        v.wait_ge(sem["l%d_" % h], 16)
+        v.tensor_scalar(T.lst[:, 64 * h:64 * h + 64], T["l%d" % h][:, 0:64], 128.0, None, A.subtract).then_inc(sem["d%d" % h], 1)
+    v.wait_ge(sem.d1, 1)
+    for j in range(3):
+        v.wait_ge(sem["ld%d" % j], 16)
+    v.wait_ge(sem.xin, n_xin)
+    for j in range(2):
+        v.tensor_copy(T.yb[:, 1024 + 512 * j:1536 + 512 * j],
+                      T.xw[:, :].indirect(T.lst[:, 64 + 32 * j:96 + 32 * j])).then_inc(sem["gv%d" % j], 1)
+
+    te.wait_ge(sem.zb_, 1)
+    te.wait_ge(sem.kb_, 1)
+    for u in range(8):
+        m = te.matmul(T.kps[:, 0:16], T.zb[:, 112 - 16 * u:240 - 16 * u], T.kb[:, u:128:8], u == 0, u == 7)
+    m.then_inc(sem.kp_, 1)
+    te.wait_ge(sem.ones_, 1)
+    te.wait_ge(sem.tri2, 1)
+    for k in range(NK):
+        if k % kq == 0:
+            te.wait_ge(sem["i%d" % (k // kq)], kq)
+            te.wait_ge(sem["s%d" % (k // kq)], 1)
+        h = k // 8
+        z = T["z%d" % h][:, k % 8:512:8]
+        te.matmul(z, T.ones[:, 0:128], T.run[:, 64 * k:64 * k + 64], True, False)
+        te.matmul(z, T.tri[:, :], T.hot[:, 64 * k:64 * k + 64], False, True).then_inc(sem["z%d_" % h], 1)
+    te.wait_ge(sem.g_, 1)
+    te.wait_ge(sem.sc, 1)
+    for h in range(2):
+        for i in range(16):
+            lo = base + 1024 * h
+            te.matmul(T["l%d" % h][:, 0:64], T.gw[:, 15 - i:143 - i], T.win[:, lo + i:lo + 1024:16],
+                      i == 0, i == 15).then_inc(sem["l%d_" % h], 1)
+
+    for j in range(3):
+        sc.wait_ge(sem["ld%d" % j], 16)
+    sc.wait_ge(sem.d0, 1)
+    sc.wait_ge(sem.xin, n_xin)
+    for j in range(2):
+        sc.activation(T.yb[:, 512 * j:512 * j + 512], T.xw[:, :].indirect(T.lst[:, 32 * j:32 * j + 32]),
+                      F.Copy).then_inc(sem["gs%d" % j], 1)
+    sc.wait_ge(sem.gs1, 1)
+    sc.dma_start(T.y[:, 512:1024], T.yb[:, 512:1024]).then_inc(sem.st2, 16)
+    sc.wait_ge(sem.st2, 16)
+
+    sy.wait_ge(sem.v_, 1)
+    sy.wait_ge(sem.vb_, 1)
+    sy.dma_start(T.val[1:128:16, :], T.vb[:, :]).then_inc(sem.vd, 16)
+    for name, a in (("gs0", 0), ("gv0", 1024), ("gv1", 1536)):
+        sy.wait_ge(sem[name], 1)
+        sy.dma_start(T.y[:, a:a + 512], T.yb[:, a:a + 512]).then_inc(sem.st, 16)
+    sy.wait_ge(sem.st, 48)

@@ -4,52 +4,55 @@ from concourse.mybir import AluOpType as A, ActivationFunctionType as F
 W = 2048
 NK = 16
 BIG = 16384.0
-CH = [(0, 768), (768, 1536), (1536, 2048)]
-NQ = 4
+TOP = 1048576.0
+PA, PB, PC = (0, 1024), (1024, 1792), (1792, 2048)
+KG = [(0, 2), (2, 6), (6, 10), (10, 14), (14, 16)]
 
 SCRATCH = {
+    "xa": ("dram", [128, PA[1] - PA[0]], "bfloat16"),
+    "xb": ("dram", [128, PB[1] - PB[0]], "bfloat16"),
     "xw": ("sbuf", [128, 4 * W], "bfloat16"),
-    "hb": ("sbuf", [128, W], "bfloat16"),
     "yb": ("sbuf", [128, W], "bfloat16"),
     "win": ("sbuf", [128, 4 * W], "bfloat16"),
-    "kraw": ("sbuf", [16, 128], "int32"),
-    "kb": ("sbuf", [16, 128], "bfloat16"),
-    "kall": ("sbuf", [128, 64], "bfloat16"),
-    "ones": ("sbuf", [128, 240], "bfloat16"),
-    "zb": ("sbuf", [16, 240], "bfloat16"),
+    "kraw": ("sbuf", [32, 128], "int32"),
+    "kb": ("sbuf", [32, 64], "bfloat16"),
+    "kall": ("sbuf", [128, 128], "bfloat16"),
+    "ones": ("sbuf", [128, 128], "bfloat16"),
+    "zb": ("sbuf", [32, 32], "bfloat16"),
     "tri": ("sbuf", [128, 128], "bfloat16"),
-    "mask8": ("sbuf", [128, 512], "bfloat16"),
-    "pul": ("sbuf", [128, 1024], "bfloat16"),
-    "mask16": ("sbuf", [8, 1024], "bfloat16"),
-    "vi": ("sbuf", [8, 1024], "bfloat16"),
-    "vb": ("sbuf", [8, 1024], "bfloat16"),
+    "mask4": ("sbuf", [128, 256], "bfloat16"),
+    "d0b": ("sbuf", [128, 512], "bfloat16"),
+    "d1b": ("sbuf", [128, 512], "bfloat16"),
     "val": ("sbuf", [128, 1024], "bfloat16"),
     "gz": ("sbuf", [128, 144], "bfloat16"),
     "gw": ("sbuf", [128, 144], "bfloat16"),
     "pc": ("sbuf", [128, 1], "int32"),
     "pq": ("sbuf", [128, 1], "int32"),
-    "pc16": ("sbuf", [128, 1], "float32"),
     "wa": ("sbuf", [128, 1], "float32"),
     "wb": ("sbuf", [128, 1], "float32"),
+    "wd": ("sbuf", [128, 1], "float32"),
+    "we": ("sbuf", [128, 1], "float32"),
     "wc": ("sbuf", [128, 1], "float32"),
     "hot": ("sbuf", [128, 1024], "bfloat16"),
     "run": ("sbuf", [128, 1024], "bfloat16"),
-    "r0": ("sbuf", [128, 512], "float32"),
-    "r1": ("sbuf", [128, 512], "float32"),
-    "pm": ("sbuf", [128, 64], "float32"),
+    "hug": ("sbuf", [128, 64], "bfloat16"),
+    "m1": ("sbuf", [128, 64], "float32"),
+    "md": ("sbuf", [128, 320], "float32"),
     "off": ("sbuf", [128, 64], "uint16"),
     "lst": ("sbuf", [128, 128], "uint16"),
     "kps": ("psum", [128, 512], "float32"),
-    "z0": ("psum", [128, 512], "float32"),
-    "z1": ("psum", [128, 512], "float32"),
     "l0": ("psum", [128, 512], "float32"),
     "l1": ("psum", [128, 512], "float32"),
 }
-SEMAPHORES = (["kl", "ld0", "ld1", "ld2", "kin", "xin", "hin0", "hin1", "sent"]
-              + ["ones_", "tri0", "tri1", "tri2", "zb_", "pc_", "c1", "c2", "v_", "kb_", "kp_", "ko", "vi_", "vb_", "vd",
-                 "win_", "q_", "w_", "w2", "g_", "z0_", "z1_", "r_", "pm_", "off_", "sc", "l0_", "l1_", "d0", "d1",
-                 "gs0", "gs1", "gv0", "gv1", "st", "st2"]
-              + ["i%d" % q for q in range(NQ)] + ["s%d" % q for q in range(NQ)])
+for _q in range(4):
+    SCRATCH["r%d" % _q] = ("sbuf", [128, 320 if _q == 3 else 256], "float32")
+    SCRATCH["z%d" % _q] = ("psum", [128, 512], "float32")
+SEMAPHORES = (["kl", "lda", "ldb", "ldc", "ldo", "tin", "cst", "kin", "xin", "hb", "sent", "ks"]
+              + ["ones_", "tri0", "tri1", "tri2", "zb_", "pc_", "c1", "c2", "c3", "kb_", "kp_", "ko", "dup_",
+                 "win_", "hug_", "md_", "q_", "w_", "w2", "w3", "r_", "m1_", "m2_", "off_", "sc", "l0_",
+                 "l1_", "d0", "d1", "gh0", "gh1", "st"]
+              + ["z%d_" % q for q in range(4)]
+              + ["i%d" % q for q in range(len(KG))] + ["s%d" % q for q in range(len(KG))])
 
 
 def dst(topo, c):
@@ -57,9 +60,13 @@ def dst(topo, c):
     return DstId(rid=rid, pnc=pid)
 
 
-def helper_of(topo, cores, src, far):
+def helpers_of(topo, cores, src, far):
     return [c for c in range(128) if topo.chip(c) == topo.chip(far) and topo.die(c) == topo.die(src)
-            and c not in cores][0]
+            and c not in cores][:2]
+
+
+def count(mask):
+    return bin(mask).count("1")
 
 
 def rank_program(g, core, T, topo):
@@ -70,24 +77,90 @@ def rank_program(g, core, T, topo):
         member_program(g, core, T, topo, cores)
 
 
+def make_mask4(g, T):
+    v, sem = g.vector, T.sem
+    v.memset(T.mask4[:, :], 1.0).then_inc(sem.c1, 1)
+    v.wait_ge(sem.c1, 1)
+    v.memset(T.mask4[:, 0:256:4], 0.0).then_inc(sem.c3, 1)
+    return T.mask4[:, :]
+
+
+def make_columns(g, T):
+    v, sem = g.vector, T.sem
+    g.iota(T.pc[:, :], [[1, 1]], 0, 1).then_inc(sem.pc_, 1)
+    v.wait_ge(sem.pc_, 1)
+    v.tensor_scalar(T.pq[:, :], T.pc[:, :], 15, None, A.bitwise_and).then_inc(sem.q_, 1)
+    v.wait_ge(sem.q_, 1)
+    v.tensor_scalar(T.wa[:, :], T.pq[:, :], 0.0, None, A.is_equal).then_inc(sem.w_, 1)
+    v.tensor_scalar(T.wb[:, :], T.pq[:, :], 1.0, None, A.is_equal).then_inc(sem.w_, 1)
+    v.tensor_scalar(T.wd[:, :], T.pq[:, :], 1.0, None, A.not_equal).then_inc(sem.w_, 1)
+    v.wait_ge(sem.w_, 3)
+
+
+def make_gw(g, T):
+    v, sem = g.vector, T.sem
+    v.memset(T.gz[:, :], 0.0).then_inc(sem.c1, 1)
+    make_columns(g, T)
+    v.tensor_scalar(T.wc[:, :], T.wa[:, :], 128.0, T.wb[:, 0:1], A.mult, A.add).then_inc(sem.w2, 1)
+    v.wait_ge(sem.c1, 1)
+    v.memset(T.gz[:, 15:144:16], 1.0).then_inc(sem.c2, 1)
+    v.wait_ge(sem.c2, 1)
+    v.wait_ge(sem.w2, 1)
+    v.tensor_scalar(T.gw[:, :], T.gz[:, :], T.wc[:, 0:1], None, A.mult).then_inc(sem.c3, 1)
+    return T.gw[:, :]
+
+
+def make_names(g, T, h):
+    v, sem = g.vector, T.sem
+    v.memset(T.d0b[:, :], 1.0).then_inc(sem.c1, 1)
+    make_columns(g, T)
+    v.tensor_scalar(T.we[:, :], T.pc[:, :], 1.0, T.wb[:, 0:1], A.subtract, A.mult).then_inc(sem.w2, 1)
+    v.wait_ge(sem.c1, 1)
+    v.tensor_scalar(T.d1b[:, :], T.d0b[:, :], T.wb[:, 0:1], None, A.mult).then_inc(sem.q_, 1)
+    v.wait_ge(sem.w2, 1)
+    v.tensor_tensor(T.wc[:, :], T.we[:, :], T.wa[:, :], A.add).then_inc(sem.w3, 1)
+    v.wait_ge(sem.q_, 2)
+    v.memset(T.gz[:, 0:32], 1.0).then_inc(sem.ones_, 1)
+    v.wait_ge(sem.w3, 1)
+    v.wait_ge(sem.ones_, 1)
+    v.tensor_scalar(T.d0b[:, 0:512:16], T.gz[:, 0:32], T.wd[:, 0:1], None, A.mult).then_inc(sem.c2, 1)
+    v.tensor_scalar(T.d1b[:, 0:512:16], T.gz[:, 0:32], T.wc[:, 0:1], None, A.mult).then_inc(sem.c2, 1)
+    v.wait_ge(sem.c2, 2)
+    out = T.val[:, 512 * h:512 * h + 512]
+    v.tensor_tensor_scan(out, T.d0b[:, :], T.d1b[:, :], 32.0 * h, A.mult, A.add).then_inc(sem.c3, 1)
+    return out
+
+
 def helper_program(g, core, T, topo, cores):
     here = [c for c in cores if topo.chip(c) == topo.chip(core)]
     if not here:
         return
-    srcs = [s for s in cores if topo.chip(s) != topo.chip(core) and helper_of(topo, cores, s, here[0]) == core]
-    sem = T.sem
-    n = 0
-    for s in srcs:
+    srcs = [s for s in cores if topo.chip(s) != topo.chip(core)]
+    for j, s in enumerate(srcs):
+        hs = helpers_of(topo, cores, s, here[0])
+        if core not in hs:
+            continue
+        k = hs.index(core)
         r = T.rank_of(s)
-        for j, (a, b) in enumerate(CH[:2]):
-            g.wait_ge(sem["hin%d" % j], 8)
-            d = T.xw[:, W * r + a:W * r + b]
+        m = topo.mask(core, here[0])
+
+        def send(src, d, rs):
             g.remote_dma_fused([RemoteDMATransfer(
-                src=T.hb[:, a:b], dsts=[d for _ in here], dst_ids=[dst(topo, c) for c in here],
-                dma_engine_mask=topo.mask(core, here[0]), remote_sem=sem.xin)], local_sem=sem.sent)
-            n += 16
-    if n:
-        g.wait_ge(sem.sent, n)
+                src=src, dsts=[d for _ in here], dst_ids=[dst(topo, c) for c in here],
+                dma_engine_mask=m, remote_sem=rs)], local_sem=T.sem.sent)
+
+        if k == 0:
+            table = make_names(g, T, j)
+        elif j == 0:
+            table = make_mask4(g, T)
+        else:
+            table = make_gw(g, T)
+        g.wait_ge(T.sem.c3, 1)
+        send(table, table, T.sem.cst)
+        buf, (a, b) = (("xa", PA), ("xb", PB))[k]
+        g.wait_ge(T.sem.hb, count(topo.mask(s, core)))
+        send(T[buf][:, :], T.xw[:, W * r + a:W * r + b], T.sem.xin)
+        g.wait_ge(T.sem.sent, 2 * count(m))
 
 
 def member_program(g, core, T, topo, cores):
@@ -96,124 +169,148 @@ def member_program(g, core, T, topo, cores):
     v, te, sc, sy = g.vector, g.tensor, g.scalar, g.sync
     mate = [c for c in cores if c != core and topo.chip(c) == topo.chip(core)][0]
     far = [c for c in cores if topo.chip(c) != topo.chip(core)]
-    helper = helper_of(topo, cores, core, far[0])
+    hs = helpers_of(topo, cores, core, far[0])
+    m_all = topo.mask(core, mate)
     m_off = topo.mask(core, far[0])
-    m_on = topo.mask(core, mate) & ~m_off
-    n_off, n_on = bin(m_off).count("1"), bin(m_on).count("1")
+    m_on = m_all & ~m_off
+    n_off, n_on, n_all = count(m_off), count(m_on), count(m_all)
+    n_help = count(topo.mask(hs[0], hs[1]))
     base = W * r
+    tc = 0 if r < T.rank_of(mate) else 64
+    tri_own = T.tri[:, tc:tc + 64]
 
-    sc.dma_start(T.kraw[:, :], T.key[:, :]).then_inc(sem.kl, 16)
-    for j, (a, b) in enumerate(CH):
-        sy.dma_start(T.xw[:, base + a:base + b], T.x[:, a:b]).then_inc(sem["ld%d" % j], 16)
+    def mine(piece):
+        return T.xw[:, base + piece[0]:base + piece[1]]
 
-    g.wait_ge(sem.ones_, 1)
-    g.affine_select(T.zb[:, :], T.ones[0:16, :], [[1, 240]], A.is_equal, 0.0, -112, -1).then_inc(sem.zb_, 1)
-    g.iota(T.pc[:, :], [[1, 1]], 0, 1).then_inc(sem.pc_, 1)
-    g.iota(T.pc16[:, :], [[1, 1]], 0, 16, allow_small_or_imprecise_dtypes=True).then_inc(sem.pc_, 1)
     g.wait_ge(sem.tri0, 1)
-    g.affine_select(T.tri[:, :], T.tri[:, :], [[-1, 128]], A.is_gt, 0.0, 0, 1).then_inc(sem.tri1, 1)
+    g.affine_select(tri_own, tri_own, [[-1, 64]], A.is_gt, 0.0, -tc, 1).then_inc(sem.tri1, 1)
+    g.wait_ge(sem.ones_, 1)
+    g.affine_select(T.zb[:, :], T.ones[0:32, 0:32], [[-1, 32]], A.is_equal, 0.0, 0, 1).then_inc(sem.zb_, 1)
     g.wait_ge(sem.tri1, 1)
-    g.affine_select(T.tri[:, :], T.tri[:, :], [[-1, 128]], A.not_equal, BIG, 0, 1).then_inc(sem.tri2, 1)
+    g.affine_select(tri_own, tri_own, [[-1, 64]], A.not_equal, BIG, -tc, 1).then_inc(sem.tri2, 1)
+    g.wait_ge(sem.tri2, 1)
+    g.remote_dma_fused([RemoteDMATransfer(src=tri_own, dst=tri_own, dst_ids=[dst(topo, mate)],
+                                          dma_engine_mask=m_all, remote_sem=sem.tin)], local_sem=sem.sent)
     g.wait_ge(sem.ko, 1)
     own = T.kall[:, 16 * r:16 * r + 16]
-    g.remote_dma_fused([RemoteDMATransfer(src=own, dsts=[own, own, own], dst_ids=[dst(topo, c) for c in far + [mate]],
-                                          dma_engine_mask=m_off, remote_sem=sem.kin)], local_sem=sem.sent)
-    n = n_off
-    for j, (a, b) in enumerate(CH):
-        g.wait_ge(sem["ld%d" % j], 16)
-        src = T.xw[:, base + a:base + b]
-        if j < 2:
-            t1 = RemoteDMATransfer(src=src, dst=T.hb[:, a:b], dst_ids=[dst(topo, helper)], dma_engine_mask=m_off,
-                                   remote_sem=sem["hin%d" % j])
-        else:
-            t1 = RemoteDMATransfer(src=src, dsts=[src, src], dst_ids=[dst(topo, c) for c in far], dma_engine_mask=m_off,
-                                   remote_sem=sem.xin)
-        t2 = RemoteDMATransfer(src=src, dst=src, dst_ids=[dst(topo, mate)], dma_engine_mask=m_on, remote_sem=sem.xin)
-        g.remote_dma_fused([t1, t2], local_sem=sem.sent)
-        n += n_off + n_on
-    g.wait_ge(sem.sent, n)
-    n_xin = 3 * n_on + 2 * (2 * 16 + n_off)
+    g.remote_dma_fused([RemoteDMATransfer(src=own, dsts=[own, own], dst_ids=[dst(topo, c) for c in far],
+                                          dma_engine_mask=m_off, remote_sem=sem.kin),
+                        RemoteDMATransfer(src=own, dst=own, dst_ids=[dst(topo, mate)],
+                                          dma_engine_mask=m_on, remote_sem=sem.kin)], local_sem=sem.ks)
+    for k, (buf, ld, piece) in enumerate((("xa", "lda", PA), ("xb", "ldb", PB))):
+        g.wait_ge(sem[ld], 16)
+        g.remote_dma_fused([RemoteDMATransfer(src=T[buf][:, :], dst=T[buf][:, :], dst_ids=[dst(topo, hs[k])],
+                                              dma_engine_mask=m_off, remote_sem=sem.hb),
+                            RemoteDMATransfer(src=T[buf][:, :], dst=mine(piece), dst_ids=[dst(topo, mate)],
+                                              dma_engine_mask=m_on, remote_sem=sem.xin)], local_sem=sem.sent)
+    g.wait_ge(sem.ldc, 16)
+    last = mine(PC)
+    g.remote_dma_fused([RemoteDMATransfer(src=last, dsts=[last, last], dst_ids=[dst(topo, c) for c in far],
+                                          dma_engine_mask=m_off, remote_sem=sem.xin),
+                        RemoteDMATransfer(src=last, dst=last, dst_ids=[dst(topo, mate)],
+                                          dma_engine_mask=m_on, remote_sem=sem.xin)], local_sem=sem.sent)
+    g.wait_ge(sem.sent, 3 * (n_off + n_on) + n_all)
+    n_xin = 3 * n_on + 2 * 2 * n_help + 2 * n_off
 
+    def wait_x(q):
+        q.wait_ge(sem.ldc, 16)
+        q.wait_ge(sem.ldo, 16)
+        q.wait_ge(sem.xin, n_xin)
+
+    v.memset(tri_own, -1.0).then_inc(sem.tri0, 1)
     v.memset(T.ones[:, :], 1.0).then_inc(sem.ones_, 1)
-    v.memset(T.tri[:, :], -1.0).then_inc(sem.tri0, 1)
-    v.memset(T.mask8[:, :], 1.0).then_inc(sem.c1, 1)
-    v.memset(T.pul[:, :], 0.0).then_inc(sem.c1, 1)
-    v.memset(T.mask16[:, :], 1.0).then_inc(sem.c1, 1)
-    v.memset(T.gz[:, :], 0.0).then_inc(sem.c1, 1)
-    v.wait_ge(sem.c1, 4)
-    v.memset(T.mask8[:, 0:512:8], 0.0).then_inc(sem.c2, 1)
-    v.memset(T.pul[:, 0:1024:16], 1.0).then_inc(sem.c2, 1)
-    v.memset(T.mask16[:, 0:1024:16], 0.0).then_inc(sem.c2, 1)
-    v.memset(T.gz[:, 15:144:16], 1.0).then_inc(sem.c2, 1)
-    v.wait_ge(sem.kl, 16)
-    v.tensor_copy(T.kb[:, :], T.kraw[:, :]).then_inc(sem.kb_, 1)
-    v.wait_ge(sem.c2, 4)
-    v.tensor_tensor_scan(T.val[:, :], T.pul[:, :], T.pul[:, :], 0.0, A.add, A.max).then_inc(sem.v_, 1)
-    v.wait_ge(sem.kp_, 1)
-    v.tensor_copy(own, T.kps[:, 0:16]).then_inc(sem.ko, 1)
-    v.tensor_tensor_scan(T.vi[:, :], T.mask16[:, :], T.mask16[:, :], 0.0, A.mult, A.add).then_inc(sem.vi_, 1)
-    v.wait_ge(sem.pc_, 2)
-    v.tensor_scalar(T.pq[:, :], T.pc[:, :], 15, None, A.bitwise_and).then_inc(sem.q_, 1)
-    v.wait_ge(sem.vi_, 1)
-    v.tensor_scalar(T.vb[:, :], T.vi[:, :], T.pc16[0:8, 0:1], None, A.add).then_inc(sem.vb_, 1)
-    v.wait_ge(sem.q_, 1)
-    v.tensor_scalar(T.wa[:, :], T.pq[:, :], 0.0, 128.0, A.is_equal, A.mult).then_inc(sem.w_, 1)
-    v.tensor_scalar(T.wb[:, :], T.pq[:, :], 1.0, None, A.is_equal).then_inc(sem.w_, 1)
-    v.wait_ge(sem.w_, 2)
-    v.tensor_tensor(T.wc[:, :], T.wa[:, :], T.wb[:, :], A.add).then_inc(sem.w2, 1)
+    v.memset(T.hug[:, :], 1024.0).then_inc(sem.hug_, 1)
     v.memset(T.win[:, base:base + W], 0.0).then_inc(sem.win_, 1)
-    v.wait_ge(sem.w2, 1)
-    v.tensor_scalar(T.gw[:, :], T.gz[:, :], T.wc[:, 0:1], None, A.mult).then_inc(sem.g_, 1)
+    v.wait_ge(sem.kl, 32)
+    v.tensor_copy(T.kb[:, :], T.kraw[:, 0:127:2]).then_inc(sem.kb_, 1)
+    v.wait_ge(sem.kp_, 4)
+    v.tensor_copy(own, T.kps[:, 0:16]).then_inc(sem.ko, 1)
+    v.memset(T.md[:, :], TOP).then_inc(sem.md_, 1)
     v.wait_ge(sem.ko, 1)
-    v.wait_ge(sem.kin, 3 * n_off)
-    kq = NK // NQ
-    for q in range(NQ):
-        for k in range(kq * q, kq * q + kq):
-            v.tensor_scalar(T.hot[:, 64 * k:64 * k + 64], T.kall[:, :], float(k), None, A.is_equal).then_inc(sem["i%d" % q], 1)
-        v.wait_ge(sem["i%d" % q], kq)
+    v.wait_ge(sem.kin, 2 * n_off + n_on)
+    for k in range(2):
+        v.tensor_scalar(T.hot[:, 64 * k:64 * k + 64], T.kall[:, 0:64], float(k), None, A.is_equal).then_inc(sem.i0, 1)
+    v.tensor_scalar(T.kall[:, 64:128], T.kall[:, 0:64], 1.0, None, A.subtract).then_inc(sem.dup_, 1)
+
+    def hots(q):
+        for k in range(KG[q][0], KG[q][1], 2):
+            v.tensor_scalar(T.hot[:, 64 * k:64 * k + 128], T.kall[:, :], float(k), None,
+                            A.is_equal).then_inc(sem["i%d" % q], 1)
+
+    def n_hot(q):
+        return 2 if q == 0 else (KG[q][1] - KG[q][0]) // 2
+
+    def scan(q):
+        v.wait_ge(sem["i%d" % q], n_hot(q))
         if q:
             v.wait_ge(sem["s%d" % (q - 1)], 1)
-        lo, hi = 64 * kq * q, 64 * kq * (q + 1)
+        lo, hi = 64 * KG[q][0], 64 * KG[q][1]
         v.tensor_tensor_scan(T.run[:, lo:hi], T.hot[:, lo:hi], T.hot[:, lo:hi],
                              T.run[:, lo - 1:lo] if q else 0.0, A.add, A.max).then_inc(sem["s%d" % q], 1)
-    for h in range(2):
-        v.wait_ge(sem["z%d_" % h], 8)
-        v.tensor_tensor_scan(T["r%d" % h][:, :], T.mask8[:, :], T["z%d" % h][:, :], 0.0, A.mult, A.max).then_inc(sem.r_, 1)
+
+    scan(0)
+    v.wait_ge(sem.dup_, 1)
+    hots(1)
+    hots(2)
+    scan(1)
+    hots(3)
+    scan(2)
+    hots(4)
+    scan(3)
+    scan(4)
+    v.wait_ge(sem.cst, 4 * n_help)
+
+    def pick(q):
+        v.wait_ge(sem["z%d_" % q], 4)
+        v.tensor_tensor_scan(T["r%d" % q][:, :], T.mask4[:, :], T["z%d" % q][:, 0:256], 0.0, A.mult, A.max
+                             ).then_inc(sem.r_, 1)
+
+    pick(0)
+    pick(1)
     v.wait_ge(sem.r_, 2)
-    v.tensor_tensor(T.pm[:, :], T.r0[:, 7:512:8], T.r1[:, 7:512:8], A.max).then_inc(sem.pm_, 1)
-    v.wait_ge(sem.pm_, 1)
-    v.tensor_scalar(T.off[:, :], T.pm[:, :], BIG + 1.0, None, A.subtract).then_inc(sem.off_, 1)
-    v.wait_ge(sem.off_, 1)
+    v.tensor_tensor(T.m1[:, :], T.r0[:, 3:256:4], T.r1[:, 3:256:4], A.max).then_inc(sem.m1_, 1)
+    pick(2)
+    v.wait_ge(sem.m1_, 1)
+    v.wait_ge(sem.md_, 1)
+    v.wait_ge(sem.r_, 3)
+    v.tensor_tensor(T.md[:, 0:320:5], T.m1[:, :], T.r2[:, 3:256:4], A.max).then_inc(sem.m2_, 1)
+    v.wait_ge(sem.m2_, 1)
+    v.wait_ge(sem.z3_, 5)
+    v.tensor_tensor_scan(T.r3[:, :], T.md[:, :], T.z3[:, 0:320], TOP, A.min, A.max).then_inc(sem.r_, 1)
+    v.wait_ge(sem.r_, 4)
+    v.tensor_scalar(T.off[:, :], T.r3[:, 3:320:5], BIG + 1.0, None, A.subtract).then_inc(sem.off_, 1)
     v.wait_ge(sem.win_, 1)
-    v.wait_ge(sem.vd, 16)
+    v.wait_ge(sem.off_, 1)
     v.tensor_copy(T.win[:, :].indirect(T.off[:, 0:64]), T.val[:, :]).then_inc(sem.sc, 1)
     for h in range(2):
         v.wait_ge(sem["l%d_" % h], 16)
-        v.tensor_scalar(T.lst[:, 64 * h:64 * h + 64], T["l%d" % h][:, 0:64], 128.0, None, A.subtract).then_inc(sem["d%d" % h], 1)
-    v.wait_ge(sem.d1, 1)
-    for j in range(3):
-        v.wait_ge(sem["ld%d" % j], 16)
-    v.wait_ge(sem.xin, n_xin)
-    for j in range(2):
-        v.tensor_copy(T.yb[:, 1024 + 512 * j:1536 + 512 * j],
-                      T.xw[:, :].indirect(T.lst[:, 64 + 32 * j:96 + 32 * j])).then_inc(sem["gv%d" % j], 1)
+        v.tensor_scalar(T.lst[:, 64 * h:64 * h + 64], T["l%d" % h][:, 0:64], 128.0, None,
+                        A.subtract).then_inc(sem["d%d" % h], 1)
+        v.wait_ge(sem["d%d" % h], 1)
+        if h == 0:
+            wait_x(v)
+        v.tensor_copy(T.yb[:, 1024 * h:1024 * h + 512],
+                      T.xw[:, :].indirect(T.lst[:, 64 * h:64 * h + 32])).then_inc(sem["gh%d" % h], 1)
 
     te.wait_ge(sem.zb_, 1)
     te.wait_ge(sem.kb_, 1)
-    for u in range(8):
-        m = te.matmul(T.kps[:, 0:16], T.zb[:, 112 - 16 * u:240 - 16 * u], T.kb[:, u:128:8], u == 0, u == 7)
-    m.then_inc(sem.kp_, 1)
+    for w in range(4):
+        te.matmul(T.kps[32 * w:32 * w + 32, 0:16], T.zb[:, :], T.kb[:, w:64:4], True, True).then_inc(sem.kp_, 1)
     te.wait_ge(sem.ones_, 1)
+    te.wait_ge(sem.hug_, 1)
+    te.matmul(T.z3[:, 4:320:5], T.ones[:, :], T.hug[:, :], True, True).then_inc(sem.z3_, 1)
     te.wait_ge(sem.tri2, 1)
-    for k in range(NK):
-        if k % kq == 0:
-            te.wait_ge(sem["i%d" % (k // kq)], kq)
-            te.wait_ge(sem["s%d" % (k // kq)], 1)
-        h = k // 8
-        z = T["z%d" % h][:, k % 8:512:8]
-        te.matmul(z, T.ones[:, 0:128], T.run[:, 64 * k:64 * k + 64], True, False)
-        te.matmul(z, T.tri[:, :], T.hot[:, 64 * k:64 * k + 64], False, True).then_inc(sem["z%d_" % h], 1)
-    te.wait_ge(sem.g_, 1)
+    te.wait_ge(sem.tin, n_all)
+    for q, (k0, k1) in enumerate(KG):
+        te.wait_ge(sem["i%d" % q], n_hot(q))
+        for k in range(k0, k1):
+            h = k // 4
+            z = T["z%d" % h][:, k % 4:320:5] if h == 3 else T["z%d" % h][:, k % 4:256:4]
+            te.matmul(z, T.tri[:, :], T.hot[:, 64 * k:64 * k + 64], True, False)
+            if k == k0:
+                te.wait_ge(sem["s%d" % q], 1)
+            te.matmul(z, T.ones[:, :], T.run[:, 64 * k:64 * k + 64], False, True).then_inc(sem["z%d_" % h], 1)
+    te.wait_ge(sem.cst, 4 * n_help)
     te.wait_ge(sem.sc, 1)
     for h in range(2):
         for i in range(16):
@@ -221,21 +318,22 @@ def member_program(g, core, T, topo, cores):
             te.matmul(T["l%d" % h][:, 0:64], T.gw[:, 15 - i:143 - i], T.win[:, lo + i:lo + 1024:16],
                       i == 0, i == 15).then_inc(sem["l%d_" % h], 1)
 
-    for j in range(3):
-        sc.wait_ge(sem["ld%d" % j], 16)
-    sc.wait_ge(sem.d0, 1)
-    sc.wait_ge(sem.xin, n_xin)
-    for j in range(2):
-        sc.activation(T.yb[:, 512 * j:512 * j + 512], T.xw[:, :].indirect(T.lst[:, 32 * j:32 * j + 32]),
-                      F.Copy).then_inc(sem["gs%d" % j], 1)
-    sc.wait_ge(sem.gs1, 1)
-    sc.dma_start(T.y[:, 512:1024], T.yb[:, 512:1024]).then_inc(sem.st2, 16)
-    sc.wait_ge(sem.st2, 16)
+    sc.dma_start(T.kraw[0:16, :], T.key[:, :]).then_inc(sem.kl, 16)
+    sc.dma_start(T.xa[:, :], T.x[:, PA[0]:PA[1]]).then_inc(sem.lda, 16)
+    sc.wait_ge(sem.ks, n_off + n_on)
+    sc.dma_start(last, T.x[:, PC[0]:PC[1]]).then_inc(sem.ldc, 16)
+    for h in range(2):
+        sc.wait_ge(sem["d%d" % h], 1)
+        if h == 0:
+            wait_x(sc)
+        sc.activation(T.yb[:, 1024 * h + 512:1024 * h + 1024],
+                      T.xw[:, :].indirect(T.lst[:, 64 * h + 32:64 * h + 64]), F.Copy).then_inc(sem["gh%d" % h], 1)
 
-    sy.wait_ge(sem.v_, 1)
-    sy.wait_ge(sem.vb_, 1)
-    sy.dma_start(T.val[1:128:16, :], T.vb[:, :]).then_inc(sem.vd, 16)
-    for name, a in (("gs0", 0), ("gv0", 1024), ("gv1", 1536)):
-        sy.wait_ge(sem[name], 1)
-        sy.dma_start(T.y[:, a:a + 512], T.yb[:, a:a + 512]).then_inc(sem.st, 16)
-    sy.wait_ge(sem.st, 48)
+    sy.dma_start(T.kraw[16:32, 0:127], T.key[:, 1:128]).then_inc(sem.kl, 16)
+    sy.wait_ge(sem.ks, n_off + n_on)
+    sy.dma_start(T.xb[:, :], T.x[:, PB[0]:PB[1]]).then_inc(sem.ldb, 16)
+    sy.dma_start(T.xw[:, base:base + PC[0]], T.x[:, 0:PC[0]]).then_inc(sem.ldo, 16)
+    for h in range(2):
+        sy.wait_ge(sem["gh%d" % h], 2)
+        sy.dma_start(T.y[:, 1024 * h:1024 * h + 1024], T.yb[:, 1024 * h:1024 * h + 1024]).then_inc(sem.st, 16)
+    sy.wait_ge(sem.st, 32)

from concourse.bass import DstId, RemoteDMATransfer
from concourse.mybir import AluOpType as A, ActivationFunctionType as F

W = 2048
NK = 16
BIG = 16384.0
TOP = 1048576.0
PA, PB, PC = (0, 1024), (1024, 1792), (1792, 2048)
KG = [(0, 2), (2, 6), (6, 10), (10, 14), (14, 16)]

SCRATCH = {
    "xa": ("dram", [128, PA[1] - PA[0]], "bfloat16"),
    "xb": ("dram", [128, PB[1] - PB[0]], "bfloat16"),
    "xw": ("sbuf", [128, 4 * W], "bfloat16"),
    "yb": ("sbuf", [128, W], "bfloat16"),
    "win": ("sbuf", [128, 4 * W], "bfloat16"),
    "kraw": ("sbuf", [32, 128], "int32"),
    "kb": ("sbuf", [32, 64], "bfloat16"),
    "kall": ("sbuf", [128, 128], "bfloat16"),
    "ones": ("sbuf", [128, 128], "bfloat16"),
    "zb": ("sbuf", [32, 32], "bfloat16"),
    "tri": ("sbuf", [128, 128], "bfloat16"),
    "mask4": ("sbuf", [128, 256], "bfloat16"),
    "d0b": ("sbuf", [128, 512], "bfloat16"),
    "d1b": ("sbuf", [128, 512], "bfloat16"),
    "val": ("sbuf", [128, 1024], "bfloat16"),
    "gz": ("sbuf", [128, 144], "bfloat16"),
    "gw": ("sbuf", [128, 144], "bfloat16"),
    "pc": ("sbuf", [128, 1], "int32"),
    "pq": ("sbuf", [128, 1], "int32"),
    "wa": ("sbuf", [128, 1], "float32"),
    "wb": ("sbuf", [128, 1], "float32"),
    "wd": ("sbuf", [128, 1], "float32"),
    "we": ("sbuf", [128, 1], "float32"),
    "wc": ("sbuf", [128, 1], "float32"),
    "hot": ("sbuf", [128, 1024], "bfloat16"),
    "run": ("sbuf", [128, 1024], "bfloat16"),
    "hug": ("sbuf", [128, 64], "bfloat16"),
    "m1": ("sbuf", [128, 64], "float32"),
    "md": ("sbuf", [128, 320], "float32"),
    "off": ("sbuf", [128, 64], "uint16"),
    "lst": ("sbuf", [128, 128], "uint16"),
    "kps": ("psum", [128, 512], "float32"),
    "l0": ("psum", [128, 512], "float32"),
    "l1": ("psum", [128, 512], "float32"),
}
for _q in range(4):
    SCRATCH["r%d" % _q] = ("sbuf", [128, 320 if _q == 3 else 256], "float32")
    SCRATCH["z%d" % _q] = ("psum", [128, 512], "float32")
SEMAPHORES = (["kl", "lda", "ldb", "ldc", "ldo", "tin", "cst", "kin", "xin", "hb", "sent", "ks"]
              + ["ones_", "tri0", "tri1", "tri2", "zb_", "pc_", "c1", "c2", "c3", "kb_", "kp_", "ko", "dup_",
                 "win_", "hug_", "md_", "q_", "w_", "w2", "w3", "r_", "m1_", "m2_", "off_", "sc", "l0_",
                 "l1_", "d0", "d1", "gh0", "gh1", "st"]
              + ["z%d_" % q for q in range(4)]
              + ["i%d" % q for q in range(len(KG))] + ["s%d" % q for q in range(len(KG))])


def dst(topo, c):
    rid, pid, _ = topo.addr(c)
    return DstId(rid=rid, pnc=pid)


def helpers_of(topo, cores, src, far):
    return [c for c in range(128) if topo.chip(c) == topo.chip(far) and topo.die(c) == topo.die(src)
            and c not in cores][:2]


def count(mask):
    return bin(mask).count("1")


def rank_program(g, core, T, topo):
    cores = list(T.cores)
    if T.rank_of(core) is None:
        helper_program(g, core, T, topo, cores)
    else:
        member_program(g, core, T, topo, cores)


def make_mask4(g, T):
    v, sem = g.vector, T.sem
    v.memset(T.mask4[:, :], 1.0).then_inc(sem.c1, 1)
    v.wait_ge(sem.c1, 1)
    v.memset(T.mask4[:, 0:256:4], 0.0).then_inc(sem.c3, 1)
    return T.mask4[:, :]


def make_columns(g, T):
    v, sem = g.vector, T.sem
    g.iota(T.pc[:, :], [[1, 1]], 0, 1).then_inc(sem.pc_, 1)
    v.wait_ge(sem.pc_, 1)
    v.tensor_scalar(T.pq[:, :], T.pc[:, :], 15, None, A.bitwise_and).then_inc(sem.q_, 1)
    v.wait_ge(sem.q_, 1)
    v.tensor_scalar(T.wa[:, :], T.pq[:, :], 0.0, None, A.is_equal).then_inc(sem.w_, 1)
    v.tensor_scalar(T.wb[:, :], T.pq[:, :], 1.0, None, A.is_equal).then_inc(sem.w_, 1)
    v.tensor_scalar(T.wd[:, :], T.pq[:, :], 1.0, None, A.not_equal).then_inc(sem.w_, 1)
    v.wait_ge(sem.w_, 3)


def make_gw(g, T):
    v, sem = g.vector, T.sem
    v.memset(T.gz[:, :], 0.0).then_inc(sem.c1, 1)
    make_columns(g, T)
    v.tensor_scalar(T.wc[:, :], T.wa[:, :], 128.0, T.wb[:, 0:1], A.mult, A.add).then_inc(sem.w2, 1)
    v.wait_ge(sem.c1, 1)
    v.memset(T.gz[:, 15:144:16], 1.0).then_inc(sem.c2, 1)
    v.wait_ge(sem.c2, 1)
    v.wait_ge(sem.w2, 1)
    v.tensor_scalar(T.gw[:, :], T.gz[:, :], T.wc[:, 0:1], None, A.mult).then_inc(sem.c3, 1)
    return T.gw[:, :]


def make_names(g, T, h):
    v, sem = g.vector, T.sem
    v.memset(T.d0b[:, :], 1.0).then_inc(sem.c1, 1)
    make_columns(g, T)
    v.tensor_scalar(T.we[:, :], T.pc[:, :], 1.0, T.wb[:, 0:1], A.subtract, A.mult).then_inc(sem.w2, 1)
    v.wait_ge(sem.c1, 1)
    v.tensor_scalar(T.d1b[:, :], T.d0b[:, :], T.wb[:, 0:1], None, A.mult).then_inc(sem.q_, 1)
    v.wait_ge(sem.w2, 1)
    v.tensor_tensor(T.wc[:, :], T.we[:, :], T.wa[:, :], A.add).then_inc(sem.w3, 1)
    v.wait_ge(sem.q_, 2)
    v.memset(T.gz[:, 0:32], 1.0).then_inc(sem.ones_, 1)
    v.wait_ge(sem.w3, 1)
    v.wait_ge(sem.ones_, 1)
    v.tensor_scalar(T.d0b[:, 0:512:16], T.gz[:, 0:32], T.wd[:, 0:1], None, A.mult).then_inc(sem.c2, 1)
    v.tensor_scalar(T.d1b[:, 0:512:16], T.gz[:, 0:32], T.wc[:, 0:1], None, A.mult).then_inc(sem.c2, 1)
    v.wait_ge(sem.c2, 2)
    out = T.val[:, 512 * h:512 * h + 512]
    v.tensor_tensor_scan(out, T.d0b[:, :], T.d1b[:, :], 32.0 * h, A.mult, A.add).then_inc(sem.c3, 1)
    return out


def helper_program(g, core, T, topo, cores):
    here = [c for c in cores if topo.chip(c) == topo.chip(core)]
    if not here:
        return
    srcs = [s for s in cores if topo.chip(s) != topo.chip(core)]
    for j, s in enumerate(srcs):
        hs = helpers_of(topo, cores, s, here[0])
        if core not in hs:
            continue
        k = hs.index(core)
        r = T.rank_of(s)
        m = topo.mask(core, here[0])

        def send(src, d, rs):
            g.remote_dma_fused([RemoteDMATransfer(
                src=src, dsts=[d for _ in here], dst_ids=[dst(topo, c) for c in here],
                dma_engine_mask=m, remote_sem=rs)], local_sem=T.sem.sent)

        if k == 0:
            table = make_names(g, T, j)
        elif j == 0:
            table = make_mask4(g, T)
        else:
            table = make_gw(g, T)
        g.wait_ge(T.sem.c3, 1)
        send(table, table, T.sem.cst)
        buf, (a, b) = (("xa", PA), ("xb", PB))[k]
        g.wait_ge(T.sem.hb, count(topo.mask(s, core)))
        send(T[buf][:, :], T.xw[:, W * r + a:W * r + b], T.sem.xin)
        g.wait_ge(T.sem.sent, 2 * count(m))


def member_program(g, core, T, topo, cores):
    r = T.rank_of(core)
    sem = T.sem
    v, te, sc, sy = g.vector, g.tensor, g.scalar, g.sync
    mate = [c for c in cores if c != core and topo.chip(c) == topo.chip(core)][0]
    far = [c for c in cores if topo.chip(c) != topo.chip(core)]
    hs = helpers_of(topo, cores, core, far[0])
    m_all = topo.mask(core, mate)
    m_off = topo.mask(core, far[0])
    m_on = m_all & ~m_off
    n_off, n_on, n_all = count(m_off), count(m_on), count(m_all)
    n_help = count(topo.mask(hs[0], hs[1]))
    base = W * r
    tc = 0 if r < T.rank_of(mate) else 64
    tri_own = T.tri[:, tc:tc + 64]

    def mine(piece):
        return T.xw[:, base + piece[0]:base + piece[1]]

    g.wait_ge(sem.tri0, 1)
    g.affine_select(tri_own, tri_own, [[-1, 64]], A.is_gt, 0.0, -tc, 1).then_inc(sem.tri1, 1)
    g.wait_ge(sem.ones_, 1)
    g.affine_select(T.zb[:, :], T.ones[0:32, 0:32], [[-1, 32]], A.is_equal, 0.0, 0, 1).then_inc(sem.zb_, 1)
    g.wait_ge(sem.tri1, 1)
    g.affine_select(tri_own, tri_own, [[-1, 64]], A.not_equal, BIG, -tc, 1).then_inc(sem.tri2, 1)
    g.wait_ge(sem.tri2, 1)
    g.remote_dma_fused([RemoteDMATransfer(src=tri_own, dst=tri_own, dst_ids=[dst(topo, mate)],
                                          dma_engine_mask=m_all, remote_sem=sem.tin)], local_sem=sem.sent)
    g.wait_ge(sem.ko, 1)
    own = T.kall[:, 16 * r:16 * r + 16]
    g.remote_dma_fused([RemoteDMATransfer(src=own, dsts=[own, own], dst_ids=[dst(topo, c) for c in far],
                                          dma_engine_mask=m_off, remote_sem=sem.kin),
                        RemoteDMATransfer(src=own, dst=own, dst_ids=[dst(topo, mate)],
                                          dma_engine_mask=m_on, remote_sem=sem.kin)], local_sem=sem.ks)
    for k, (buf, ld, piece) in enumerate((("xa", "lda", PA), ("xb", "ldb", PB))):
        g.wait_ge(sem[ld], 16)
        g.remote_dma_fused([RemoteDMATransfer(src=T[buf][:, :], dst=T[buf][:, :], dst_ids=[dst(topo, hs[k])],
                                              dma_engine_mask=m_off, remote_sem=sem.hb),
                            RemoteDMATransfer(src=T[buf][:, :], dst=mine(piece), dst_ids=[dst(topo, mate)],
                                              dma_engine_mask=m_on, remote_sem=sem.xin)], local_sem=sem.sent)
    g.wait_ge(sem.ldc, 16)
    last = mine(PC)
    g.remote_dma_fused([RemoteDMATransfer(src=last, dsts=[last, last], dst_ids=[dst(topo, c) for c in far],
                                          dma_engine_mask=m_off, remote_sem=sem.xin),
                        RemoteDMATransfer(src=last, dst=last, dst_ids=[dst(topo, mate)],
                                          dma_engine_mask=m_on, remote_sem=sem.xin)], local_sem=sem.sent)
    g.wait_ge(sem.sent, 3 * (n_off + n_on) + n_all)
    n_xin = 3 * n_on + 2 * 2 * n_help + 2 * n_off

    def wait_x(q):
        q.wait_ge(sem.ldc, 16)
        q.wait_ge(sem.ldo, 16)
        q.wait_ge(sem.xin, n_xin)

    v.memset(tri_own, -1.0).then_inc(sem.tri0, 1)
    v.memset(T.ones[:, :], 1.0).then_inc(sem.ones_, 1)
    v.memset(T.hug[:, :], 1024.0).then_inc(sem.hug_, 1)
    v.memset(T.win[:, base:base + W], 0.0).then_inc(sem.win_, 1)
    v.wait_ge(sem.kl, 32)
    v.tensor_copy(T.kb[:, :], T.kraw[:, 0:127:2]).then_inc(sem.kb_, 1)
    v.wait_ge(sem.kp_, 4)
    v.tensor_copy(own, T.kps[:, 0:16]).then_inc(sem.ko, 1)
    v.memset(T.md[:, :], TOP).then_inc(sem.md_, 1)
    v.wait_ge(sem.ko, 1)
    v.wait_ge(sem.kin, 2 * n_off + n_on)
    for k in range(2):
        v.tensor_scalar(T.hot[:, 64 * k:64 * k + 64], T.kall[:, 0:64], float(k), None, A.is_equal).then_inc(sem.i0, 1)
    v.tensor_scalar(T.kall[:, 64:128], T.kall[:, 0:64], 1.0, None, A.subtract).then_inc(sem.dup_, 1)

    def hots(q):
        for k in range(KG[q][0], KG[q][1], 2):
            v.tensor_scalar(T.hot[:, 64 * k:64 * k + 128], T.kall[:, :], float(k), None,
                            A.is_equal).then_inc(sem["i%d" % q], 1)

    def n_hot(q):
        return 2 if q == 0 else (KG[q][1] - KG[q][0]) // 2

    def scan(q):
        v.wait_ge(sem["i%d" % q], n_hot(q))
        if q:
            v.wait_ge(sem["s%d" % (q - 1)], 1)
        lo, hi = 64 * KG[q][0], 64 * KG[q][1]
        v.tensor_tensor_scan(T.run[:, lo:hi], T.hot[:, lo:hi], T.hot[:, lo:hi],
                             T.run[:, lo - 1:lo] if q else 0.0, A.add, A.max).then_inc(sem["s%d" % q], 1)

    scan(0)
    v.wait_ge(sem.dup_, 1)
    hots(1)
    hots(2)
    scan(1)
    hots(3)
    scan(2)
    hots(4)
    scan(3)
    scan(4)
    v.wait_ge(sem.cst, 4 * n_help)

    def pick(q):
        v.wait_ge(sem["z%d_" % q], 4)
        v.tensor_tensor_scan(T["r%d" % q][:, :], T.mask4[:, :], T["z%d" % q][:, 0:256], 0.0, A.mult, A.max
                             ).then_inc(sem.r_, 1)

    pick(0)
    pick(1)
    v.wait_ge(sem.r_, 2)
    v.tensor_tensor(T.m1[:, :], T.r0[:, 3:256:4], T.r1[:, 3:256:4], A.max).then_inc(sem.m1_, 1)
    pick(2)
    v.wait_ge(sem.m1_, 1)
    v.wait_ge(sem.md_, 1)
    v.wait_ge(sem.r_, 3)
    v.tensor_tensor(T.md[:, 0:320:5], T.m1[:, :], T.r2[:, 3:256:4], A.max).then_inc(sem.m2_, 1)
    v.wait_ge(sem.m2_, 1)
    v.wait_ge(sem.z3_, 5)
    v.tensor_tensor_scan(T.r3[:, :], T.md[:, :], T.z3[:, 0:320], TOP, A.min, A.max).then_inc(sem.r_, 1)
    v.wait_ge(sem.r_, 4)
    v.tensor_scalar(T.off[:, :], T.r3[:, 3:320:5], BIG + 1.0, None, A.subtract).then_inc(sem.off_, 1)
    v.wait_ge(sem.win_, 1)
    v.wait_ge(sem.off_, 1)
    v.tensor_copy(T.win[:, :].indirect(T.off[:, 0:64]), T.val[:, :]).then_inc(sem.sc, 1)
    for h in range(2):
        v.wait_ge(sem["l%d_" % h], 16)
        v.tensor_scalar(T.lst[:, 64 * h:64 * h + 64], T["l%d" % h][:, 0:64], 128.0, None,
                        A.subtract).then_inc(sem["d%d" % h], 1)
        v.wait_ge(sem["d%d" % h], 1)
        if h == 0:
            wait_x(v)
        v.tensor_copy(T.yb[:, 1024 * h:1024 * h + 512],
                      T.xw[:, :].indirect(T.lst[:, 64 * h:64 * h + 32])).then_inc(sem["gh%d" % h], 1)

    te.wait_ge(sem.zb_, 1)
    te.wait_ge(sem.kb_, 1)
    for w in range(4):
        te.matmul(T.kps[32 * w:32 * w + 32, 0:16], T.zb[:, :], T.kb[:, w:64:4], True, True).then_inc(sem.kp_, 1)
    te.wait_ge(sem.ones_, 1)
    te.wait_ge(sem.hug_, 1)
    te.matmul(T.z3[:, 4:320:5], T.ones[:, :], T.hug[:, :], True, True).then_inc(sem.z3_, 1)
    te.wait_ge(sem.tri2, 1)
    te.wait_ge(sem.tin, n_all)
    for q, (k0, k1) in enumerate(KG):
        te.wait_ge(sem["i%d" % q], n_hot(q))
        for k in range(k0, k1):
            h = k // 4
            z = T["z%d" % h][:, k % 4:320:5] if h == 3 else T["z%d" % h][:, k % 4:256:4]
            te.matmul(z, T.tri[:, :], T.hot[:, 64 * k:64 * k + 64], True, False)
            if k == k0:
                te.wait_ge(sem["s%d" % q], 1)
            te.matmul(z, T.ones[:, :], T.run[:, 64 * k:64 * k + 64], False, True).then_inc(sem["z%d_" % h], 1)
    te.wait_ge(sem.cst, 4 * n_help)
    te.wait_ge(sem.sc, 1)
    for h in range(2):
        for i in range(16):
            lo = base + 1024 * h
            te.matmul(T["l%d" % h][:, 0:64], T.gw[:, 15 - i:143 - i], T.win[:, lo + i:lo + 1024:16],
                      i == 0, i == 15).then_inc(sem["l%d_" % h], 1)

    sc.dma_start(T.kraw[0:16, :], T.key[:, :]).then_inc(sem.kl, 16)
    sc.dma_start(T.xa[:, :], T.x[:, PA[0]:PA[1]]).then_inc(sem.lda, 16)
    sc.wait_ge(sem.ks, n_off + n_on)
    sc.dma_start(last, T.x[:, PC[0]:PC[1]]).then_inc(sem.ldc, 16)
    for h in range(2):
        sc.wait_ge(sem["d%d" % h], 1)
        if h == 0:
            wait_x(sc)
        sc.activation(T.yb[:, 1024 * h + 512:1024 * h + 1024],
                      T.xw[:, :].indirect(T.lst[:, 64 * h + 32:64 * h + 64]), F.Copy).then_inc(sem["gh%d" % h], 1)

    sy.dma_start(T.kraw[16:32, 0:127], T.key[:, 1:128]).then_inc(sem.kl, 16)
    sy.wait_ge(sem.ks, n_off + n_on)
    sy.dma_start(T.xb[:, :], T.x[:, PB[0]:PB[1]]).then_inc(sem.ldb, 16)
    sy.dma_start(T.xw[:, base:base + PC[0]], T.x[:, 0:PC[0]]).then_inc(sem.ldo, 16)
    for h in range(2):
        sy.wait_ge(sem["gh%d" % h], 2)
        sy.dma_start(T.y[:, 1024 * h:1024 * h + 1024], T.yb[:, 1024 * h:1024 * h + 1024]).then_inc(sem.st, 16)
    sy.wait_ge(sem.st, 32)
